import numpy as np
CORES = [6,46,86,134,174,214,262,302,342,390,430,470]
N = 12
def setup_inputs(rng):
    return {"x": rng.standard_normal((N, 128, 48), dtype=np.float32)}
def reference(x):
    b = 48 // N
    blocks = x.reshape(N, 128, N, b)
    return {"y": np.ascontiguousarray(blocks.transpose(2, 1, 0, 3)).reshape(N, 128, 48)}

@@ -1,0 +1,46 @@
+SCRATCH = {
+    "xs": ("sbuf", [128, 48], "float32"),
+    "land": ("sbuf", [128, 48], "float32"),
+    "stage": ("sbuf", [128, 12], "float32"),
+}
+SEMAPHORES = ["loaded", "own", "sent", "fwd", "arrived", "stored"]
+
+B = 4
+E8 = 0xFF
+
+
+def rank_program(g, core, T, topo):
+    r = T.rank_of(core)
+    if r is None:
+        return
+    h, c = r // 3, r % 3
+    mate_h, cable_h, diag_h = h ^ 1, 3 - h, (h + 2) % 4
+    S = T.sem
+
+    def blk(t, j, n=1):
+        return t[:, B * j:B * (j + n)]
+
+    def send(dst_rank, out_ap, in_ap, sem):
+        d = T.cores[dst_rank]
+        rid, pid = topo.addr(d, core)
+        g.remote_dma(out_ap, in_ap, sem, S.sent, pid, rid, E8)
+
+    g.dma_start(T.xs[:], T.x[:]).then_inc(S.loaded, 16)
+    g.dma_start(blk(T.land, r), blk(T.x, r)).then_inc(S.own, 16)
+    g.wait_ge(S.loaded, 16)
+    n = 0
+    for c2 in range(3):
+        send(3 * mate_h + c2, blk(T.stage, c), blk(T.xs, 3 * diag_h + c2), S.fwd)
+        n += 1
+    for j in range(12):
+        if j != r and j // 3 != diag_h:
+            send(j, blk(T.land, r), blk(T.xs, j), S.arrived)
+            n += 1
+    g.wait_ge(S.fwd, 3 * 8)
+    send(3 * cable_h + c, blk(T.land, 3 * mate_h, 3), T.stage[:], S.arrived)
+    n += 1
+    g.wait_ge(S.arrived, 9 * 8)
+    g.wait_ge(S.own, 16)
+    g.dma_start(T.y[:], T.land[:]).then_inc(S.stored, 16)
+    g.wait_ge(S.sent, n * 8)
+    g.wait_ge(S.stored, 16)

@@ -9,38 +9,44 @@ B = 4
 E8 = 0xFF
 
 
+def blk(t, j, n=1):
+    return t[:, B * j:B * (j + n)]
+
+
 def rank_program(g, core, T, topo):
-    r = T.rank_of(core)
-    if r is None:
-        return
-    h, c = r // 3, r % 3
-    mate_h, cable_h, diag_h = h ^ 1, 3 - h, (h + 2) % 4
     S = T.sem
 
-    def blk(t, j, n=1):
-        return t[:, B * j:B * (j + n)]
-
-    def send(dst_rank, out_ap, in_ap, sem):
-        d = T.cores[dst_rank]
+    def send(d, out_ap, in_ap, sem):
         rid, pid = topo.addr(d, core)
         g.remote_dma(out_ap, in_ap, sem, S.sent, pid, rid, E8)
 
+    r = T.rank_of(core)
+    if r is None:
+        q = T.rank_of(core - 1) if core % 8 == 7 else None
+        if q is None:
+            return
+        hh, c = q // 3, q % 3
+        src = 3 * (3 - hh) + c
+        g.wait_ge(S.fwd, 8)
+        for c2 in (c + 1, c + 2, c):
+            c2 %= 3
+            send(T.cores[3 * (hh ^ 1) + c2], blk(T.land, src), blk(T.stage, c2), S.arrived)
+        g.wait_ge(S.sent, 3 * 8)
+        return
+
+    h, c = r // 3, r % 3
+    mate_h, cable_h, diag_h = h ^ 1, 3 - h, (h + 2) % 4
     g.dma_start(T.xs[:], T.x[:]).then_inc(S.loaded, 16)
     g.dma_start(blk(T.land, r), blk(T.x, r)).then_inc(S.own, 16)
     g.wait_ge(S.loaded, 16)
-    n = 0
-    for c2 in range(3):
-        send(3 * mate_h + c2, blk(T.stage, c), blk(T.xs, 3 * diag_h + c2), S.fwd)
-        n += 1
-    for j in range(12):
-        if j != r and j // 3 != diag_h:
-            send(j, blk(T.land, r), blk(T.xs, j), S.arrived)
-            n += 1
-    g.wait_ge(S.fwd, 3 * 8)
-    send(3 * cable_h + c, blk(T.land, 3 * mate_h, 3), T.stage[:], S.arrived)
-    n += 1
-    g.wait_ge(S.arrived, 9 * 8)
+    send(T.cores[3 * cable_h + c] + 1, T.stage[:], blk(T.xs, 3 * diag_h, 3), S.fwd)
+    direct = [3 * cable_h + (c + 1) % 3, 3 * cable_h + (c + 2) % 3, 3 * cable_h + c,
+              3 * mate_h + (c + 1) % 3, 3 * mate_h + (c + 2) % 3, 3 * mate_h + c,
+              3 * h + (c + 1) % 3, 3 * h + (c + 2) % 3]
+    for j in direct:
+        send(T.cores[j], blk(T.land, r), blk(T.xs, j), S.arrived)
+    g.wait_ge(S.arrived, 11 * 8)
     g.wait_ge(S.own, 16)
     g.dma_start(T.y[:], T.land[:]).then_inc(S.stored, 16)
-    g.wait_ge(S.sent, n * 8)
+    g.wait_ge(S.sent, 9 * 8)
     g.wait_ge(S.stored, 16)

@@ -1,3 +1,5 @@
+from concourse.bass import RemoteDMATransfer, DstId
+
 SCRATCH = {
     "xs": ("sbuf", [128, 48], "float32"),
     "land": ("sbuf", [128, 48], "float32"),
@@ -6,47 +8,70 @@ SCRATCH = {
 SEMAPHORES = ["loaded", "own", "sent", "fwd", "arrived", "stored"]
 
 B = 4
-E8 = 0xFF
 
 
 def blk(t, j, n=1):
     return t[:, B * j:B * (j + n)]
 
 
+def far(c):
+    return 1 if c != 1 else 0
+
+
+def engines(s, r):
+    hs, cs, hr, cr = s // 3, s % 3, r // 3, r % 3
+    if hs == hr:
+        return 2
+    if hr == (hs + 2) % 4:
+        return 8 if cr == cs else 4
+    return 2 if cr == far(cs) else 4
+
+
 def rank_program(g, core, T, topo):
     S = T.sem
 
-    def send(d, out_ap, in_ap, sem):
+    def tr(d, out_ap, in_ap, sem, mask):
         rid, pid = topo.addr(d, core)
-        g.remote_dma(out_ap, in_ap, sem, S.sent, pid, rid, E8)
+        return RemoteDMATransfer(dst_ids=[DstId(rid=rid, pnc=pid)], dma_engine_mask=mask, remote_sem=sem,
+                                 src=in_ap, dst=out_ap)
 
     r = T.rank_of(core)
     if r is None:
-        q = T.rank_of(core - 1) if core % 8 == 7 else None
-        if q is None:
+        q = T.rank_of(core - core % 8 + 6)
+        role = core % 8
+        if q is None or role not in (2, 3, 5, 7):
             return
-        hh, c = q // 3, q % 3
-        src = 3 * (3 - hh) + c
-        g.wait_ge(S.fwd, 8)
-        for c2 in (c + 1, c + 2, c):
-            c2 %= 3
-            send(T.cores[3 * (hh ^ 1) + c2], blk(T.land, src), blk(T.stage, c2), S.arrived)
-        g.wait_ge(S.sent, 3 * 8)
+        h, c = q // 3, q % 3
+        if role == 2:
+            src, th, cs = q, h ^ 1, [c2 for c2 in range(3) if c2 != far(c)]
+        elif role == 3:
+            src, th, cs = q, 3 - h, [c2 for c2 in range(3) if c2 != far(c)]
+        elif role == 7:
+            src, th, cs = 3 * (3 - h) + c, h ^ 1, [c2 for c2 in range(3) if c2 != c]
+        else:
+            src, th, cs = 3 * (3 - h) + c, h ^ 1, [c]
+        w = 8 // len(cs)
+        g.wait_ge(S.fwd, 4)
+        g.remote_dma_fused([tr(T.cores[3 * th + c2], blk(T.land, src), blk(T.stage, c2), S.arrived,
+                               ((1 << w) - 1) << (w * i)) for i, c2 in enumerate(cs)], local_sem=S.sent)
+        g.wait_ge(S.sent, 8)
         return
 
     h, c = r // 3, r % 3
     mate_h, cable_h, diag_h = h ^ 1, 3 - h, (h + 2) % 4
     g.dma_start(T.xs[:], T.x[:]).then_inc(S.loaded, 16)
-    g.dma_start(blk(T.land, r), blk(T.x, r)).then_inc(S.own, 16)
     g.wait_ge(S.loaded, 16)
-    send(T.cores[3 * cable_h + c] + 1, T.stage[:], blk(T.xs, 3 * diag_h, 3), S.fwd)
-    direct = [3 * cable_h + (c + 1) % 3, 3 * cable_h + (c + 2) % 3, 3 * cable_h + c,
-              3 * mate_h + (c + 1) % 3, 3 * mate_h + (c + 2) % 3, 3 * mate_h + c,
-              3 * h + (c + 1) % 3, 3 * h + (c + 2) % 3]
-    for j in direct:
-        send(T.cores[j], blk(T.land, r), blk(T.xs, j), S.arrived)
-    g.wait_ge(S.arrived, 11 * 8)
+    peer = T.cores[3 * cable_h + c]
+    g.remote_dma_fused([tr(peer + 1, T.stage[:], blk(T.xs, 3 * diag_h, 3), S.fwd, 0x000F),
+                        tr(peer - 1, T.stage[:], blk(T.xs, 3 * diag_h, 3), S.fwd, 0x00F0),
+                        tr(core - 4, T.stage[:], blk(T.xs, 3 * mate_h, 3), S.fwd, 0x0F00),
+                        tr(core - 3, T.stage[:], blk(T.xs, 3 * cable_h, 3), S.fwd, 0xF000)], local_sem=S.sent)
+    mine = [3 * cable_h + far(c), 3 * mate_h + far(c), 3 * h + (c + 1) % 3, 3 * h + (c + 2) % 3]
+    g.remote_dma_fused([tr(T.cores[j], blk(T.land, r), blk(T.xs, j), S.arrived, 3 << (2 * i))
+                        for i, j in enumerate(mine)], local_sem=S.sent)
+    g.dma_start(blk(T.land, r), blk(T.xs, r)).then_inc(S.own, 16)
+    g.wait_ge(S.arrived, sum(engines(s, r) for s in range(12) if s != r))
     g.wait_ge(S.own, 16)
     g.dma_start(T.y[:], T.land[:]).then_inc(S.stored, 16)
-    g.wait_ge(S.sent, 9 * 8)
+    g.wait_ge(S.sent, 16 + 8)
     g.wait_ge(S.stored, 16)

@@ -21,9 +21,11 @@ def far(c):
 def engines(s, r):
     hs, cs, hr, cr = s // 3, s % 3, r // 3, r % 3
     if hs == hr:
-        return 2
+        return 4
     if hr == (hs + 2) % 4:
         return 8 if cr == cs else 4
+    if hr == 3 - hs:
+        return 2
     return 2 if cr == far(cs) else 4
 
 
@@ -45,7 +47,7 @@ def rank_program(g, core, T, topo):
         if role == 2:
             src, th, cs = q, h ^ 1, [c2 for c2 in range(3) if c2 != far(c)]
         elif role == 3:
-            src, th, cs = q, 3 - h, [c2 for c2 in range(3) if c2 != far(c)]
+            src, th, cs = q, h, [c2 for c2 in range(3) if c2 != c]
         elif role == 7:
             src, th, cs = 3 * (3 - h) + c, h ^ 1, [c2 for c2 in range(3) if c2 != c]
         else:
@@ -65,8 +67,8 @@ def rank_program(g, core, T, topo):
     g.remote_dma_fused([tr(peer + 1, T.stage[:], blk(T.xs, 3 * diag_h, 3), S.fwd, 0x000F),
                         tr(peer - 1, T.stage[:], blk(T.xs, 3 * diag_h, 3), S.fwd, 0x00F0),
                         tr(core - 4, T.stage[:], blk(T.xs, 3 * mate_h, 3), S.fwd, 0x0F00),
-                        tr(core - 3, T.stage[:], blk(T.xs, 3 * cable_h, 3), S.fwd, 0xF000)], local_sem=S.sent)
-    mine = [3 * cable_h + far(c), 3 * mate_h + far(c), 3 * h + (c + 1) % 3, 3 * h + (c + 2) % 3]
+                        tr(core - 3, T.stage[:], blk(T.xs, 3 * h, 3), S.fwd, 0xF000)], local_sem=S.sent)
+    mine = [3 * cable_h, 3 * cable_h + 1, 3 * cable_h + 2, 3 * mate_h + far(c)]
     g.remote_dma_fused([tr(T.cores[j], blk(T.land, r), blk(T.xs, j), S.arrived, 3 << (2 * i))
                         for i, j in enumerate(mine)], local_sem=S.sent)
     g.dma_start(blk(T.land, r), blk(T.xs, r)).then_inc(S.own, 16)

from concourse.bass import RemoteDMATransfer, DstId

SCRATCH = {
    "xs": ("sbuf", [128, 48], "float32"),
    "land": ("sbuf", [128, 48], "float32"),
    "stage": ("sbuf", [128, 12], "float32"),
}
SEMAPHORES = ["loaded", "own", "sent", "fwd", "arrived", "stored"]

B = 4


def blk(t, j, n=1):
    return t[:, B * j:B * (j + n)]


def far(c):
    return 1 if c != 1 else 0


def engines(s, r):
    hs, cs, hr, cr = s // 3, s % 3, r // 3, r % 3
    if hs == hr:
        return 4
    if hr == (hs + 2) % 4:
        return 8 if cr == cs else 4
    if hr == 3 - hs:
        return 2
    return 2 if cr == far(cs) else 4


def rank_program(g, core, T, topo):
    S = T.sem

    def tr(d, out_ap, in_ap, sem, mask):
        rid, pid = topo.addr(d, core)
        return RemoteDMATransfer(dst_ids=[DstId(rid=rid, pnc=pid)], dma_engine_mask=mask, remote_sem=sem,
                                 src=in_ap, dst=out_ap)

    r = T.rank_of(core)
    if r is None:
        q = T.rank_of(core - core % 8 + 6)
        role = core % 8
        if q is None or role not in (2, 3, 5, 7):
            return
        h, c = q // 3, q % 3
        if role == 2:
            src, th, cs = q, h ^ 1, [c2 for c2 in range(3) if c2 != far(c)]
        elif role == 3:
            src, th, cs = q, h, [c2 for c2 in range(3) if c2 != c]
        elif role == 7:
            src, th, cs = 3 * (3 - h) + c, h ^ 1, [c2 for c2 in range(3) if c2 != c]
        else:
            src, th, cs = 3 * (3 - h) + c, h ^ 1, [c]
        w = 8 // len(cs)
        g.wait_ge(S.fwd, 4)
        g.remote_dma_fused([tr(T.cores[3 * th + c2], blk(T.land, src), blk(T.stage, c2), S.arrived,
                               ((1 << w) - 1) << (w * i)) for i, c2 in enumerate(cs)], local_sem=S.sent)
        g.wait_ge(S.sent, 8)
        return

    h, c = r // 3, r % 3
    mate_h, cable_h, diag_h = h ^ 1, 3 - h, (h + 2) % 4
    g.dma_start(T.xs[:], T.x[:]).then_inc(S.loaded, 16)
    g.wait_ge(S.loaded, 16)
    peer = T.cores[3 * cable_h + c]
    g.remote_dma_fused([tr(peer + 1, T.stage[:], blk(T.xs, 3 * diag_h, 3), S.fwd, 0x000F),
                        tr(peer - 1, T.stage[:], blk(T.xs, 3 * diag_h, 3), S.fwd, 0x00F0),
                        tr(core - 4, T.stage[:], blk(T.xs, 3 * mate_h, 3), S.fwd, 0x0F00),
                        tr(core - 3, T.stage[:], blk(T.xs, 3 * h, 3), S.fwd, 0xF000)], local_sem=S.sent)
    mine = [3 * cable_h, 3 * cable_h + 1, 3 * cable_h + 2, 3 * mate_h + far(c)]
    g.remote_dma_fused([tr(T.cores[j], blk(T.land, r), blk(T.xs, j), S.arrived, 3 << (2 * i))
                        for i, j in enumerate(mine)], local_sem=S.sent)
    g.dma_start(blk(T.land, r), blk(T.xs, r)).then_inc(S.own, 16)
    g.wait_ge(S.arrived, sum(engines(s, r) for s in range(12) if s != r))
    g.wait_ge(S.own, 16)
    g.dma_start(T.y[:], T.land[:]).then_inc(S.stored, 16)
    g.wait_ge(S.sent, 16 + 8)
    g.wait_ge(S.stored, 16)
